import numpy as np, ml_dtypes
CORES = [56,61,80,85]
N = 4
import mx_ref
NC, GR, GC, T = 512, 2, 2, 2
TA, TB = T // GC, T // GR
BF = ml_dtypes.bfloat16
def setup_inputs(rng):
    def f(*shape):
        return mx_ref.flush((rng.standard_normal(shape, dtype=np.float32) * np.exp2(rng.integers(-2, 3, shape[:-1] + (1,)))).astype(BF))
    return {"a": f(N, 128, TA * 512), "b": f(N, 128, TB * 4 * NC)}
def setup_inputs_blocks(rng):
    d = setup_inputs(rng)
    for k in ("a", "b"): d[k] = mx_ref.spread(d[k], rng, 1)
    return d
def setup_inputs_wide(rng):
    d = setup_inputs(rng)
    for k in ("a", "b"): d[k] = mx_ref.flush((d[k].astype(np.float32) * np.exp2(rng.integers(-8, 9, (N, 1, 1))).astype(np.float32)).astype(BF))
    return d
def setup_inputs_zeros(rng):
    d = setup_inputs(rng); v = d["b"].reshape(N, 128, -1, 4).copy()
    v[np.broadcast_to((rng.random((N, 1, v.shape[2], 1)) < 0.33), v.shape)] = 0
    d["b"] = v.reshape(d["b"].shape)
    return d
def reference(a, b):
    A = lambda i, s: mx_ref.quantize(a[i * GC + s // TA][:, 512 * (s % TA):512 * (s % TA) + 512])
    B = lambda s, j: mx_ref.quantize(b[(s // TB) * GC + j][:, 4 * NC * (s % TB):4 * NC * (s % TB) + 4 * NC])
    y = np.zeros((N, 128, NC), np.float32)
    for r in range(N):
        for s in range(T):
            p = mx_ref.matmul(A(r // GC, s), B(s, r % GC))
            y[r] = p if s == 0 else y[r] + p
    return {"y": y}

@@ -1,0 +1,189 @@
+from concourse.bass import DstId, RemoteDMATransfer
+from concourse.mybir import dt, ActivationFunctionType
+
+GR, GC = 2, 2
+NC = 512
+MA = 128
+HALF = NC // 2
+GRP = 128
+BANK = 512
+
+E_FAR = 4
+E_NEAR = 4
+E_FWD = 4
+E_ROW = 4
+
+SCRATCH = {
+    "abf": ("sbuf", [128, 4 * MA], "bfloat16"),
+    "bbf": ("sbuf", [128, 4 * NC], "bfloat16"),
+    "qa": ("sbuf", [128, MA], "float8_e4m3fn_x4"),
+    "sa": ("sbuf", [128, MA], "uint8"),
+    "qb": ("sbuf", [128, NC], "float8_e4m3fn_x4"),
+    "sb": ("sbuf", [128, NC], "uint8"),
+    "ra": ("sbuf", [128, MA], "float8_e4m3fn_x4"),
+    "rsa": ("sbuf", [128, MA], "uint8"),
+    "rb": ("sbuf", [128, NC], "float8_e4m3fn_x4"),
+    "rsb": ("sbuf", [128, NC], "uint8"),
+    "acc": ("psum", [128, BANK * (NC // GRP)], "float32"),
+    "yo": ("sbuf", [128, NC], "float32"),
+}
+SEMAPHORES = ["ldb0", "ldb1", "lda", "qb0", "qb1", "qa", "sent", "hop", "arrA", "arrS", "arrF", "arrN",
+              "mm0", "mm1", "mm2", "mm3", "cp0", "cp1", "cp2", "cp3", "st0", "st1"]
+
+
+def _bits(mask):
+    return [k for k in range(16) if (mask >> k) & 1]
+
+
+def _mask(bits):
+    m = 0
+    for k in bits:
+        m |= 1 << k
+    return m
+
+
+def _spread(bits, n):
+    step = max(1, len(bits) // n)
+    return bits[0::step][:n]
+
+
+def _ways(topo, cores, src, dst):
+    every = range(topo.CHIPS * topo.CORES_PER_CHIP)
+    ok = [c for c in every if c not in cores and topo.die(c) == topo.die(src)
+          and topo.may_write(src, c) and topo.may_write(c, dst)]
+    near = [c for c in ok if topo.chip(c) == topo.chip(src)]
+    far = [c for c in ok if topo.same_plane(topo.chip(src), topo.chip(c)) and topo.mates(topo.chip(c), topo.chip(dst))]
+    return near, far
+
+
+def _codes(buf, lo, hi):
+    return buf[:, lo:hi].bitcast(dt.uint8)
+
+
+def _pass_on(g, T, topo, core, dst, view, n_in, sem_out):
+    rid, pid, _ = topo.addr(dst)
+    eng = _spread(_bits(topo.mask(core, dst)), E_FWD)
+    g.wait_ge(T.sem.hop, n_in)
+    g.remote_dma(out_ap=view, in_ap=view, remote_sem=sem_out, local_sem=T.sem.sent, pid=pid, routing_id=rid,
+                 dma_engine_mask=_mask(eng))
+    g.wait_ge(T.sem.sent, len(eng))
+
+
+def rank_program(g, core, T, topo):
+    S = T.sem
+    cores = list(T.cores)
+    rank = T.rank_of(core)
+
+    if rank is None:
+        for r, src in enumerate(cores):
+            dst = cores[(r + GC) % (GR * GC)]
+            near, far = _ways(topo, cores, src, dst)
+            if core == far[0]:
+                _pass_on(g, T, topo, core, dst, _codes(T.rb, 0, HALF), E_FAR, S.arrF)
+            elif core == near[0]:
+                _pass_on(g, T, topo, core, dst, _codes(T.rb, HALF, NC), 2 * E_NEAR, S.arrN)
+            elif core == near[1]:
+                _pass_on(g, T, topo, core, dst, T.rsb[:, 0:NC], E_NEAR, S.arrS)
+        return
+
+    row, col = rank // GC, rank % GC
+    nbr = cores[row * GC + (1 - col)]
+    peer = cores[(1 - row) * GC + col]
+    near, far = _ways(topo, cores, core, peer)
+
+    g.sync.dma_start(T.bbf[:, 0:4 * HALF], T.b[:, 0:4 * HALF]).then_inc(S.ldb0, 16)
+    g.sync.dma_start(T.bbf[:, 4 * HALF:4 * NC], T.b[:, 4 * HALF:4 * NC]).then_inc(S.ldb1, 16)
+    g.sync.dma_start(T.abf[:], T.a[:]).then_inc(S.lda, 16)
+
+    v = g.vector
+    v.wait_ge(S.ldb0, 16)
+    v.quantize_mx(T.qb[:, 0:HALF], T.sb[:, 0:HALF], T.bbf[:, 0:4 * HALF]).then_inc(S.qb0, 1)
+    v.wait_ge(S.ldb1, 16)
+    v.quantize_mx(T.qb[:, HALF:NC], T.sb[:, HALF:NC], T.bbf[:, 4 * HALF:4 * NC]).then_inc(S.qb1, 1)
+    v.wait_ge(S.lda, 16)
+    v.quantize_mx(T.qa[:], T.sa[:], T.abf[:]).then_inc(S.qa, 1)
+
+    off = _bits(topo.mask(core, far[0]))
+    on = _bits(topo.mask(core, near[0]))
+    e_far = _spread(off, E_FAR)
+    pool = [k for k in on if k not in off] + [k for k in off if k not in e_far]
+    e_n = [pool[i * E_NEAR:(i + 1) * E_NEAR] for i in range(3)]
+    sent = 0
+
+    rid, pid, _ = topo.addr(far[0])
+    g.wait_ge(S.qb0, 1)
+    g.remote_dma(out_ap=_codes(T.rb, 0, HALF), in_ap=_codes(T.qb, 0, HALF), remote_sem=S.hop, local_sem=S.sent,
+                 pid=pid, routing_id=rid, dma_engine_mask=_mask(e_far))
+    sent += len(e_far)
+
+    mid = (HALF + NC) // 2
+    rid0, pid0, _ = topo.addr(near[0])
+    rid1, pid1, _ = topo.addr(near[1])
+    g.wait_ge(S.qb1, 1)
+    g.remote_dma_fused([
+        RemoteDMATransfer(dst_ids=[DstId(rid=rid0, pnc=pid0)], dma_engine_mask=_mask(e_n[0]), remote_sem=S.hop,
+                          src=_codes(T.qb, HALF, mid), dst=_codes(T.rb, HALF, mid)),
+        RemoteDMATransfer(dst_ids=[DstId(rid=rid0, pnc=pid0)], dma_engine_mask=_mask(e_n[1]), remote_sem=S.hop,
+                          src=_codes(T.qb, mid, NC), dst=_codes(T.rb, mid, NC)),
+        RemoteDMATransfer(dst_ids=[DstId(rid=rid1, pnc=pid1)], dma_engine_mask=_mask(e_n[2]), remote_sem=S.hop,
+                          src=T.sb[:, 0:NC], dst=T.rsb[:, 0:NC]),
+    ], local_sem=S.sent)
+    sent += 3 * E_NEAR
+
+    rid, pid, _ = topo.addr(nbr)
+    ok = _bits(topo.mask(core, nbr))
+    e_a = [[k for k in e if k in ok][:E_ROW] for e in e_n[:2]]
+    g.wait_ge(S.qa, 1)
+    g.remote_dma(out_ap=_codes(T.ra, 0, MA), in_ap=_codes(T.qa, 0, MA), remote_sem=S.arrA, local_sem=S.sent,
+                 pid=pid, routing_id=rid, dma_engine_mask=_mask(e_a[0]))
+    g.remote_dma(out_ap=T.rsa[:, 0:MA], in_ap=T.sa[:, 0:MA], remote_sem=S.arrA, local_sem=S.sent,
+                 pid=pid, routing_id=rid, dma_engine_mask=_mask(e_a[1]))
+    sent += len(e_a[0]) + len(e_a[1])
+    g.wait_ge(S.sent, sent)
+
+    t = g.tensor
+    own_a, nbr_a = (T.qa[:], T.sa[:]), (T.ra[:], T.rsa[:])
+
+    def wait_a(which):
+        if which is own_a:
+            t.wait_ge(S.qa, 1)
+        else:
+            t.wait_ge(S.arrA, 2 * E_ROW)
+
+    a_first = own_a if col == row else nbr_a
+    a_second = nbr_a if col == row else own_a
+    groups = range(NC // GRP)
+    t.wait_ge(S.qb0, 1)
+    t.wait_ge(S.qb1, 1)
+    wait_a(a_first)
+    for k in groups:
+        t.matmul_mx(T.acc[:, BANK * k:BANK * k + GRP], a_first[0], a_first[1],
+                    T.qb[:, GRP * k:GRP * (k + 1)], T.sb[:, GRP * k:GRP * (k + 1)], True, False)
+    wait_a(a_second)
+    t.wait_ge(S.arrS, E_FWD)
+    for k in groups:
+        if GRP * k == 0:
+            t.wait_ge(S.arrF, E_FWD)
+        if GRP * k == HALF:
+            t.wait_ge(S.arrN, E_FWD)
+        t.matmul_mx(T.acc[:, BANK * k:BANK * k + GRP], a_second[0], a_second[1],
+                    T.rb[:, GRP * k:GRP * (k + 1)], T.rsb[:, GRP * k:GRP * (k + 1)], False, True
+                    ).then_inc(S["mm%d" % k], 1)
+
+    sc = g.scalar
+    for k in groups:
+        out, src = T.yo[:, GRP * k:GRP * (k + 1)], T.acc[:, BANK * k:BANK * k + GRP]
+        if k % 2 == 0:
+            v.wait_ge(S["mm%d" % k], 1)
+            v.tensor_copy(out, src).then_inc(S["cp%d" % k], 1)
+        else:
+            sc.wait_ge(S["mm%d" % k], 1)
+            sc.activation(out, src, ActivationFunctionType.Copy).then_inc(S["cp%d" % k], 1)
+    g.sync.wait_ge(S.cp0, 1)
+    g.sync.wait_ge(S.cp1, 1)
+    g.sync.dma_start(T.y[:, 0:HALF], T.yo[:, 0:HALF]).then_inc(S.st0, 16)
+    sc.wait_ge(S.cp2, 1)
+    sc.wait_ge(S.cp3, 1)
+    sc.dma_start(T.y[:, HALF:NC], T.yo[:, HALF:NC]).then_inc(S.st1, 16)
+    g.sync.wait_ge(S.st0, 16)
+    sc.wait_ge(S.st1, 16)

@@ -1,17 +1,13 @@
 from concourse.bass import DstId, RemoteDMATransfer
-from concourse.mybir import dt, ActivationFunctionType
+from concourse.mybir import dt
 
 GR, GC = 2, 2
 NC = 512
 MA = 128
-HALF = NC // 2
 GRP = 128
 BANK = 512
-
-E_FAR = 4
-E_NEAR = 4
+NG = NC // GRP
 E_FWD = 4
-E_ROW = 4
 
 SCRATCH = {
     "abf": ("sbuf", [128, 4 * MA], "bfloat16"),
@@ -24,11 +20,12 @@ SCRATCH = {
     "rsa": ("sbuf", [128, MA], "uint8"),
     "rb": ("sbuf", [128, NC], "float8_e4m3fn_x4"),
     "rsb": ("sbuf", [128, NC], "uint8"),
-    "acc": ("psum", [128, BANK * (NC // GRP)], "float32"),
+    "acc": ("psum", [128, BANK * NG], "float32"),
     "yo": ("sbuf", [128, NC], "float32"),
 }
-SEMAPHORES = ["ldb0", "ldb1", "lda", "qb0", "qb1", "qa", "sent", "hop", "arrA", "arrS", "arrF", "arrN",
-              "mm0", "mm1", "mm2", "mm3", "cp0", "cp1", "cp2", "cp3", "st0", "st1"]
+SEMAPHORES = ["ld0", "ld1", "ld2", "lda", "q0", "q1", "q2", "qa", "sent", "hop", "hop2", "arrA", "arrS",
+              "arr0", "arr1", "arr2", "arr3", "mm0", "mm1", "mm2", "mm3", "cp0", "cp1", "cp2", "cp3",
+              "st0", "st1", "st2", "st3"]
 
 
 def _bits(mask):
@@ -42,31 +39,32 @@ def _mask(bits):
     return m
 
 
-def _spread(bits, n):
-    step = max(1, len(bits) // n)
-    return bits[0::step][:n]
-
-
-def _ways(topo, cores, src, dst):
+def _plan(topo, cores, src, dst):
     every = range(topo.CHIPS * topo.CORES_PER_CHIP)
     ok = [c for c in every if c not in cores and topo.die(c) == topo.die(src)
           and topo.may_write(src, c) and topo.may_write(c, dst)]
     near = [c for c in ok if topo.chip(c) == topo.chip(src)]
     far = [c for c in ok if topo.same_plane(topo.chip(src), topo.chip(c)) and topo.mates(topo.chip(c), topo.chip(dst))]
-    return near, far
+    off = _bits(topo.mask(src, far[0]))
+    stay = [k for k in _bits(topo.mask(src, near[0])) if k not in off]
+    h = len(stay) // 2
+    return {"P": near[1], "Q": near[0], "F1": far[0], "F2": far[1],
+            "e0": stay, "e1": off[0::2], "e2": off[1::2], "e3": stay[:h], "eS": stay[h:]}
 
 
-def _codes(buf, lo, hi):
-    return buf[:, lo:hi].bitcast(dt.uint8)
+def _codes(buf, k):
+    return buf[:, GRP * k:GRP * (k + 1)].bitcast(dt.uint8)
 
 
-def _pass_on(g, T, topo, core, dst, view, n_in, sem_out):
+def _pass_on(g, T, topo, core, dst, steps):
     rid, pid, _ = topo.addr(dst)
-    eng = _spread(_bits(topo.mask(core, dst)), E_FWD)
-    g.wait_ge(T.sem.hop, n_in)
-    g.remote_dma(out_ap=view, in_ap=view, remote_sem=sem_out, local_sem=T.sem.sent, pid=pid, routing_id=rid,
-                 dma_engine_mask=_mask(eng))
-    g.wait_ge(T.sem.sent, len(eng))
+    allowed = _bits(topo.mask(core, dst))
+    eng = allowed[0::max(1, len(allowed) // E_FWD)][:E_FWD]
+    for sem_in, n_in, view, sem_out in steps:
+        g.wait_ge(sem_in, n_in)
+        g.remote_dma(out_ap=view, in_ap=view, remote_sem=sem_out, local_sem=T.sem.sent, pid=pid, routing_id=rid,
+                     dma_engine_mask=_mask(eng))
+    g.wait_ge(T.sem.sent, len(eng) * len(steps))
 
 
 def rank_program(g, core, T, topo):
@@ -77,69 +75,54 @@ def rank_program(g, core, T, topo):
     if rank is None:
         for r, src in enumerate(cores):
             dst = cores[(r + GC) % (GR * GC)]
-            near, far = _ways(topo, cores, src, dst)
-            if core == far[0]:
-                _pass_on(g, T, topo, core, dst, _codes(T.rb, 0, HALF), E_FAR, S.arrF)
-            elif core == near[0]:
-                _pass_on(g, T, topo, core, dst, _codes(T.rb, HALF, NC), 2 * E_NEAR, S.arrN)
-            elif core == near[1]:
-                _pass_on(g, T, topo, core, dst, T.rsb[:, 0:NC], E_NEAR, S.arrS)
+            p = _plan(topo, cores, src, dst)
+            if core == p["P"]:
+                _pass_on(g, T, topo, core, dst, [(S.hop, len(p["e0"]), _codes(T.rb, 0), S.arr0),
+                                                 (S.hop2, len(p["eS"]), T.rsb[:, 0:NC], S.arrS)])
+            elif core == p["F1"]:
+                _pass_on(g, T, topo, core, dst, [(S.hop, len(p["e1"]), _codes(T.rb, 1), S.arr1)])
+            elif core == p["F2"]:
+                _pass_on(g, T, topo, core, dst, [(S.hop, len(p["e2"]), _codes(T.rb, 2), S.arr2)])
+            elif core == p["Q"]:
+                _pass_on(g, T, topo, core, dst, [(S.hop, len(p["e3"]), _codes(T.rb, 3), S.arr3)])
         return
 
     row, col = rank // GC, rank % GC
     nbr = cores[row * GC + (1 - col)]
     peer = cores[(1 - row) * GC + col]
-    near, far = _ways(topo, cores, core, peer)
+    p = _plan(topo, cores, core, peer)
 
-    g.sync.dma_start(T.bbf[:, 0:4 * HALF], T.b[:, 0:4 * HALF]).then_inc(S.ldb0, 16)
-    g.sync.dma_start(T.bbf[:, 4 * HALF:4 * NC], T.b[:, 4 * HALF:4 * NC]).then_inc(S.ldb1, 16)
+    cuts = [(0, GRP), (GRP, NC - GRP), (NC - GRP, NC)]
+    for i, (lo, hi) in enumerate(cuts):
+        g.sync.dma_start(T.bbf[:, 4 * lo:4 * hi], T.b[:, 4 * lo:4 * hi]).then_inc(S["ld%d" % i], 16)
     g.sync.dma_start(T.abf[:], T.a[:]).then_inc(S.lda, 16)
 
     v = g.vector
-    v.wait_ge(S.ldb0, 16)
-    v.quantize_mx(T.qb[:, 0:HALF], T.sb[:, 0:HALF], T.bbf[:, 0:4 * HALF]).then_inc(S.qb0, 1)
-    v.wait_ge(S.ldb1, 16)
-    v.quantize_mx(T.qb[:, HALF:NC], T.sb[:, HALF:NC], T.bbf[:, 4 * HALF:4 * NC]).then_inc(S.qb1, 1)
+    for i, (lo, hi) in enumerate(cuts):
+        v.wait_ge(S["ld%d" % i], 16)
+        v.quantize_mx(T.qb[:, lo:hi], T.sb[:, lo:hi], T.bbf[:, 4 * lo:4 * hi]).then_inc(S["q%d" % i], 1)
     v.wait_ge(S.lda, 16)
     v.quantize_mx(T.qa[:], T.sa[:], T.abf[:]).then_inc(S.qa, 1)
 
-    off = _bits(topo.mask(core, far[0]))
-    on = _bits(topo.mask(core, near[0]))
-    e_far = _spread(off, E_FAR)
-    pool = [k for k in on if k not in off] + [k for k in off if k not in e_far]
-    e_n = [pool[i * E_NEAR:(i + 1) * E_NEAR] for i in range(3)]
-    sent = 0
+    def to(dst, eng, sem, src_ap, dst_ap):
+        rid, pid, _ = topo.addr(dst)
+        return RemoteDMATransfer(dst_ids=[DstId(rid=rid, pnc=pid)], dma_engine_mask=_mask(eng), remote_sem=sem,
+                                 src=src_ap, dst=dst_ap)
 
-    rid, pid, _ = topo.addr(far[0])
-    g.wait_ge(S.qb0, 1)
-    g.remote_dma(out_ap=_codes(T.rb, 0, HALF), in_ap=_codes(T.qb, 0, HALF), remote_sem=S.hop, local_sem=S.sent,
-                 pid=pid, routing_id=rid, dma_engine_mask=_mask(e_far))
-    sent += len(e_far)
-
-    mid = (HALF + NC) // 2
-    rid0, pid0, _ = topo.addr(near[0])
-    rid1, pid1, _ = topo.addr(near[1])
-    g.wait_ge(S.qb1, 1)
-    g.remote_dma_fused([
-        RemoteDMATransfer(dst_ids=[DstId(rid=rid0, pnc=pid0)], dma_engine_mask=_mask(e_n[0]), remote_sem=S.hop,
-                          src=_codes(T.qb, HALF, mid), dst=_codes(T.rb, HALF, mid)),
-        RemoteDMATransfer(dst_ids=[DstId(rid=rid0, pnc=pid0)], dma_engine_mask=_mask(e_n[1]), remote_sem=S.hop,
-                          src=_codes(T.qb, mid, NC), dst=_codes(T.rb, mid, NC)),
-        RemoteDMATransfer(dst_ids=[DstId(rid=rid1, pnc=pid1)], dma_engine_mask=_mask(e_n[2]), remote_sem=S.hop,
-                          src=T.sb[:, 0:NC], dst=T.rsb[:, 0:NC]),
-    ], local_sem=S.sent)
-    sent += 3 * E_NEAR
-
-    rid, pid, _ = topo.addr(nbr)
-    ok = _bits(topo.mask(core, nbr))
-    e_a = [[k for k in e if k in ok][:E_ROW] for e in e_n[:2]]
+    g.wait_ge(S.q0, 1)
+    g.remote_dma_fused([to(p["P"], p["e0"], S.hop, _codes(T.qb, 0), _codes(T.rb, 0))], local_sem=S.sent)
+    g.wait_ge(S.q1, 1)
+    g.remote_dma_fused([to(p["F1"], p["e1"], S.hop, _codes(T.qb, 1), _codes(T.rb, 1)),
+                        to(p["F2"], p["e2"], S.hop, _codes(T.qb, 2), _codes(T.rb, 2))], local_sem=S.sent)
+    g.wait_ge(S.q2, 1)
+    g.remote_dma_fused([to(p["Q"], p["e3"], S.hop, _codes(T.qb, 3), _codes(T.rb, 3)),
+                        to(p["P"], p["eS"], S.hop2, T.sb[:, 0:NC], T.rsb[:, 0:NC])], local_sem=S.sent)
     g.wait_ge(S.qa, 1)
-    g.remote_dma(out_ap=_codes(T.ra, 0, MA), in_ap=_codes(T.qa, 0, MA), remote_sem=S.arrA, local_sem=S.sent,
-                 pid=pid, routing_id=rid, dma_engine_mask=_mask(e_a[0]))
-    g.remote_dma(out_ap=T.rsa[:, 0:MA], in_ap=T.sa[:, 0:MA], remote_sem=S.arrA, local_sem=S.sent,
-                 pid=pid, routing_id=rid, dma_engine_mask=_mask(e_a[1]))
-    sent += len(e_a[0]) + len(e_a[1])
-    g.wait_ge(S.sent, sent)
+    g.remote_dma_fused([to(nbr, p["e3"], S.arrA, T.qa[:, 0:MA].bitcast(dt.uint8), T.ra[:, 0:MA].bitcast(dt.uint8))],
+                       local_sem=S.sent)
+    g.remote_dma_fused([to(nbr, p["eS"], S.arrA, T.sa[:, 0:MA], T.rsa[:, 0:MA])], local_sem=S.sent)
+    n_a = len(p["e3"]) + len(p["eS"])
+    g.wait_ge(S.sent, len(p["e0"]) + len(p["e1"]) + len(p["e2"]) + len(p["e3"]) + len(p["eS"]) + n_a)
 
     t = g.tensor
     own_a, nbr_a = (T.qa[:], T.sa[:]), (T.ra[:], T.rsa[:])
@@ -148,42 +131,30 @@ def rank_program(g, core, T, topo):
         if which is own_a:
             t.wait_ge(S.qa, 1)
         else:
-            t.wait_ge(S.arrA, 2 * E_ROW)
+            t.wait_ge(S.arrA, n_a)
 
     a_first = own_a if col == row else nbr_a
     a_second = nbr_a if col == row else own_a
-    groups = range(NC // GRP)
-    t.wait_ge(S.qb0, 1)
-    t.wait_ge(S.qb1, 1)
+    for i in range(len(cuts)):
+        t.wait_ge(S["q%d" % i], 1)
     wait_a(a_first)
-    for k in groups:
+    for k in range(NG):
         t.matmul_mx(T.acc[:, BANK * k:BANK * k + GRP], a_first[0], a_first[1],
                     T.qb[:, GRP * k:GRP * (k + 1)], T.sb[:, GRP * k:GRP * (k + 1)], True, False)
     wait_a(a_second)
     t.wait_ge(S.arrS, E_FWD)
-    for k in groups:
-        if GRP * k == 0:
-            t.wait_ge(S.arrF, E_FWD)
-        if GRP * k == HALF:
-            t.wait_ge(S.arrN, E_FWD)
+    for k in range(NG):
+        t.wait_ge(S["arr%d" % k], E_FWD)
         t.matmul_mx(T.acc[:, BANK * k:BANK * k + GRP], a_second[0], a_second[1],
                     T.rb[:, GRP * k:GRP * (k + 1)], T.rsb[:, GRP * k:GRP * (k + 1)], False, True
                     ).then_inc(S["mm%d" % k], 1)
 
-    sc = g.scalar
-    for k in groups:
-        out, src = T.yo[:, GRP * k:GRP * (k + 1)], T.acc[:, BANK * k:BANK * k + GRP]
-        if k % 2 == 0:
-            v.wait_ge(S["mm%d" % k], 1)
-            v.tensor_copy(out, src).then_inc(S["cp%d" % k], 1)
-        else:
-            sc.wait_ge(S["mm%d" % k], 1)
-            sc.activation(out, src, ActivationFunctionType.Copy).then_inc(S["cp%d" % k], 1)
-    g.sync.wait_ge(S.cp0, 1)
-    g.sync.wait_ge(S.cp1, 1)
-    g.sync.dma_start(T.y[:, 0:HALF], T.yo[:, 0:HALF]).then_inc(S.st0, 16)
-    sc.wait_ge(S.cp2, 1)
-    sc.wait_ge(S.cp3, 1)
-    sc.dma_start(T.y[:, HALF:NC], T.yo[:, HALF:NC]).then_inc(S.st1, 16)
-    g.sync.wait_ge(S.st0, 16)
-    sc.wait_ge(S.st1, 16)
+    for k in range(NG):
+        v.wait_ge(S["mm%d" % k], 1)
+        v.tensor_copy(T.yo[:, GRP * k:GRP * (k + 1)], T.acc[:, BANK * k:BANK * k + GRP]).then_inc(S["cp%d" % k], 1)
+        q = g.sync if k % 2 == 0 else g.scalar
+        q.wait_ge(S["cp%d" % k], 1)
+        q.dma_start(T.y[:, GRP * k:GRP * (k + 1)], T.yo[:, GRP * k:GRP * (k + 1)]).then_inc(S["st%d" % k], 16)
+    for k in range(NG):
+        q = g.sync if k % 2 == 0 else g.scalar
+        q.wait_ge(S["st%d" % k], 16)

from concourse.bass import DstId, RemoteDMATransfer
from concourse.mybir import dt

GR, GC = 2, 2
NC = 512
MA = 128
GRP = 128
BANK = 512
NG = NC // GRP
E_FWD = 4

SCRATCH = {
    "abf": ("sbuf", [128, 4 * MA], "bfloat16"),
    "bbf": ("sbuf", [128, 4 * NC], "bfloat16"),
    "qa": ("sbuf", [128, MA], "float8_e4m3fn_x4"),
    "sa": ("sbuf", [128, MA], "uint8"),
    "qb": ("sbuf", [128, NC], "float8_e4m3fn_x4"),
    "sb": ("sbuf", [128, NC], "uint8"),
    "ra": ("sbuf", [128, MA], "float8_e4m3fn_x4"),
    "rsa": ("sbuf", [128, MA], "uint8"),
    "rb": ("sbuf", [128, NC], "float8_e4m3fn_x4"),
    "rsb": ("sbuf", [128, NC], "uint8"),
    "acc": ("psum", [128, BANK * NG], "float32"),
    "yo": ("sbuf", [128, NC], "float32"),
}
SEMAPHORES = ["ld0", "ld1", "ld2", "lda", "q0", "q1", "q2", "qa", "sent", "hop", "hop2", "arrA", "arrS",
              "arr0", "arr1", "arr2", "arr3", "mm0", "mm1", "mm2", "mm3", "cp0", "cp1", "cp2", "cp3",
              "st0", "st1", "st2", "st3"]


def _bits(mask):
    return [k for k in range(16) if (mask >> k) & 1]


def _mask(bits):
    m = 0
    for k in bits:
        m |= 1 << k
    return m


def _plan(topo, cores, src, dst):
    every = range(topo.CHIPS * topo.CORES_PER_CHIP)
    ok = [c for c in every if c not in cores and topo.die(c) == topo.die(src)
          and topo.may_write(src, c) and topo.may_write(c, dst)]
    near = [c for c in ok if topo.chip(c) == topo.chip(src)]
    far = [c for c in ok if topo.same_plane(topo.chip(src), topo.chip(c)) and topo.mates(topo.chip(c), topo.chip(dst))]
    off = _bits(topo.mask(src, far[0]))
    stay = [k for k in _bits(topo.mask(src, near[0])) if k not in off]
    h = len(stay) // 2
    return {"P": near[1], "Q": near[0], "F1": far[0], "F2": far[1],
            "e0": stay, "e1": off[0::2], "e2": off[1::2], "e3": stay[:h], "eS": stay[h:]}


def _codes(buf, k):
    return buf[:, GRP * k:GRP * (k + 1)].bitcast(dt.uint8)


def _pass_on(g, T, topo, core, dst, steps):
    rid, pid, _ = topo.addr(dst)
    allowed = _bits(topo.mask(core, dst))
    eng = allowed[0::max(1, len(allowed) // E_FWD)][:E_FWD]
    for sem_in, n_in, view, sem_out in steps:
        g.wait_ge(sem_in, n_in)
        g.remote_dma(out_ap=view, in_ap=view, remote_sem=sem_out, local_sem=T.sem.sent, pid=pid, routing_id=rid,
                     dma_engine_mask=_mask(eng))
    g.wait_ge(T.sem.sent, len(eng) * len(steps))


def rank_program(g, core, T, topo):
    S = T.sem
    cores = list(T.cores)
    rank = T.rank_of(core)

    if rank is None:
        for r, src in enumerate(cores):
            dst = cores[(r + GC) % (GR * GC)]
            p = _plan(topo, cores, src, dst)
            if core == p["P"]:
                _pass_on(g, T, topo, core, dst, [(S.hop, len(p["e0"]), _codes(T.rb, 0), S.arr0),
                                                 (S.hop2, len(p["eS"]), T.rsb[:, 0:NC], S.arrS)])
            elif core == p["F1"]:
                _pass_on(g, T, topo, core, dst, [(S.hop, len(p["e1"]), _codes(T.rb, 1), S.arr1)])
            elif core == p["F2"]:
                _pass_on(g, T, topo, core, dst, [(S.hop, len(p["e2"]), _codes(T.rb, 2), S.arr2)])
            elif core == p["Q"]:
                _pass_on(g, T, topo, core, dst, [(S.hop, len(p["e3"]), _codes(T.rb, 3), S.arr3)])
        return

    row, col = rank // GC, rank % GC
    nbr = cores[row * GC + (1 - col)]
    peer = cores[(1 - row) * GC + col]
    p = _plan(topo, cores, core, peer)

    cuts = [(0, GRP), (GRP, NC - GRP), (NC - GRP, NC)]
    for i, (lo, hi) in enumerate(cuts):
        g.sync.dma_start(T.bbf[:, 4 * lo:4 * hi], T.b[:, 4 * lo:4 * hi]).then_inc(S["ld%d" % i], 16)
    g.sync.dma_start(T.abf[:], T.a[:]).then_inc(S.lda, 16)

    v = g.vector
    for i, (lo, hi) in enumerate(cuts):
        v.wait_ge(S["ld%d" % i], 16)
        v.quantize_mx(T.qb[:, lo:hi], T.sb[:, lo:hi], T.bbf[:, 4 * lo:4 * hi]).then_inc(S["q%d" % i], 1)
    v.wait_ge(S.lda, 16)
    v.quantize_mx(T.qa[:], T.sa[:], T.abf[:]).then_inc(S.qa, 1)

    def to(dst, eng, sem, src_ap, dst_ap):
        rid, pid, _ = topo.addr(dst)
        return RemoteDMATransfer(dst_ids=[DstId(rid=rid, pnc=pid)], dma_engine_mask=_mask(eng), remote_sem=sem,
                                 src=src_ap, dst=dst_ap)

    g.wait_ge(S.q0, 1)
    g.remote_dma_fused([to(p["P"], p["e0"], S.hop, _codes(T.qb, 0), _codes(T.rb, 0))], local_sem=S.sent)
    g.wait_ge(S.q1, 1)
    g.remote_dma_fused([to(p["F1"], p["e1"], S.hop, _codes(T.qb, 1), _codes(T.rb, 1)),
                        to(p["F2"], p["e2"], S.hop, _codes(T.qb, 2), _codes(T.rb, 2))], local_sem=S.sent)
    g.wait_ge(S.q2, 1)
    g.remote_dma_fused([to(p["Q"], p["e3"], S.hop, _codes(T.qb, 3), _codes(T.rb, 3)),
                        to(p["P"], p["eS"], S.hop2, T.sb[:, 0:NC], T.rsb[:, 0:NC])], local_sem=S.sent)
    g.wait_ge(S.qa, 1)
    g.remote_dma_fused([to(nbr, p["e3"], S.arrA, T.qa[:, 0:MA].bitcast(dt.uint8), T.ra[:, 0:MA].bitcast(dt.uint8))],
                       local_sem=S.sent)
    g.remote_dma_fused([to(nbr, p["eS"], S.arrA, T.sa[:, 0:MA], T.rsa[:, 0:MA])], local_sem=S.sent)
    n_a = len(p["e3"]) + len(p["eS"])
    g.wait_ge(S.sent, len(p["e0"]) + len(p["e1"]) + len(p["e2"]) + len(p["e3"]) + len(p["eS"]) + n_a)

    t = g.tensor
    own_a, nbr_a = (T.qa[:], T.sa[:]), (T.ra[:], T.rsa[:])

    def wait_a(which):
        if which is own_a:
            t.wait_ge(S.qa, 1)
        else:
            t.wait_ge(S.arrA, n_a)

    a_first = own_a if col == row else nbr_a
    a_second = nbr_a if col == row else own_a
    for i in range(len(cuts)):
        t.wait_ge(S["q%d" % i], 1)
    wait_a(a_first)
    for k in range(NG):
        t.matmul_mx(T.acc[:, BANK * k:BANK * k + GRP], a_first[0], a_first[1],
                    T.qb[:, GRP * k:GRP * (k + 1)], T.sb[:, GRP * k:GRP * (k + 1)], True, False)
    wait_a(a_second)
    t.wait_ge(S.arrS, E_FWD)
    for k in range(NG):
        t.wait_ge(S["arr%d" % k], E_FWD)
        t.matmul_mx(T.acc[:, BANK * k:BANK * k + GRP], a_second[0], a_second[1],
                    T.rb[:, GRP * k:GRP * (k + 1)], T.rsb[:, GRP * k:GRP * (k + 1)], False, True
                    ).then_inc(S["mm%d" % k], 1)

    for k in range(NG):
        v.wait_ge(S["mm%d" % k], 1)
        v.tensor_copy(T.yo[:, GRP * k:GRP * (k + 1)], T.acc[:, BANK * k:BANK * k + GRP]).then_inc(S["cp%d" % k], 1)
        q = g.sync if k % 2 == 0 else g.scalar
        q.wait_ge(S["cp%d" % k], 1)
        q.dma_start(T.y[:, GRP * k:GRP * (k + 1)], T.yo[:, GRP * k:GRP * (k + 1)]).then_inc(S["st%d" % k], 16)
    for k in range(NG):
        q = g.sync if k % 2 == 0 else g.scalar
        q.wait_ge(S["st%d" % k], 16)
